import numpy as np
import ml_dtypes


def mxq(x, axis, fmt="e4m3"):
    dtype, down = {"e4m3": (ml_dtypes.float8_e4m3fn, 7), "e5m2": (ml_dtypes.float8_e5m2, 14)}[fmt]
    v = np.moveaxis(np.asarray(x, np.float32).astype(ml_dtypes.bfloat16).astype(np.float64), axis, -1)
    blocks = v.reshape(v.shape[:-1] + (-1, 32))
    amax = np.abs(blocks).max(-1, keepdims=True)
    byte = np.maximum(np.where(amax > 0, np.frexp(amax)[1] - 1 + 127, 0) - down, 1)
    scale = np.exp2(byte - 127.0)
    codes = (blocks / scale).astype(np.float32).astype(dtype).astype(np.float64)
    return np.moveaxis((codes * scale).reshape(v.shape), -1, axis)


WIDE = False


def mx_kscale(k):
    if not WIDE:
        return np.ones(k)
    levels = np.array([10, -10, 5, -5, 0])
    if k % 512:
        return np.exp2(np.random.permutation(np.resize(levels, k // 32))).repeat(32)
    a = np.empty((k // 512, 16))
    for p in range(k // 512):
        a[p, :8] = np.random.permutation(np.resize(levels, 8))
        for g in range(8):
            far = levels[np.abs(levels - a[p, g]) >= 10]
            a[p, g + 8] = far[np.random.randint(len(far))]
    return np.exp2(a.ravel()).repeat(32)


def f64(x):
    return np.asarray(x).astype(np.float64)


def striped8(idx):
    return np.asarray(idx).reshape(8, -1, 16).transpose(0, 2, 1).reshape(128, -1).astype(np.uint16)


def unstriped8(offs):
    return offs.reshape(8, 16, -1).transpose(0, 2, 1).reshape(8, -1).astype(np.int64)


def pick8(x, idx, run):
    r = np.arange(len(x))
    return x[r[:, None], idx[r % (8 * run) // run]]


E2M1 = np.array([0.0, 0.5, 1.0, 1.5, 2.0, 3.0, 4.0, 6.0, -0.0, -0.5, -1.0, -1.5, -2.0, -3.0, -4.0, -6.0])


def pack_weight(w, fmt):
    k, n = w.shape
    w = f64(np.asarray(w, np.float32).astype(ml_dtypes.bfloat16)).reshape(k // 32, 32, n)
    amax = np.abs(w).max(1)
    if fmt == "e4m3":
        byte = np.frexp(amax)[1] - 1 + 127 - 7
    else:
        mant, ex = np.frexp(amax / 6.0)
        byte = np.where(mant > 0.5, ex, ex - 1) + 127
    byte = np.clip(np.where(amax > 0, byte, 1), 1, 254)
    scaled = (w * np.exp2(127.0 - byte)[:, None, :]).reshape(k, n).astype(np.float32)
    by_word = np.ascontiguousarray(scaled.reshape(k // 512, 128, 4, n).transpose(0, 1, 3, 2))
    if fmt == "e4m3":
        words = by_word.astype(ml_dtypes.float8_e4m3fn).view(np.uint8)
    else:
        c = by_word.astype(ml_dtypes.float4_e2m1fn).view(np.uint8) & 0xF
        words = (c[..., 0::2] | (c[..., 1::2] << 4)).reshape(k // 512, 128, 2 * n)
    return np.ascontiguousarray(words), np.ascontiguousarray(byte.astype(np.uint8).reshape(k // 512, 16, n))


def unpack_weight(words, scales, fmt):
    g, _, n = scales.shape
    words = np.ascontiguousarray(words).reshape(g, 128, n, -1)
    if fmt == "e4m3":
        vals = words.view(ml_dtypes.float8_e4m3fn).astype(np.float64)
    else:
        nib = np.empty((g, 128, n, 4), np.uint8)
        nib[..., 0::2] = words & 0xF
        nib[..., 1::2] = words >> 4
        vals = E2M1[nib]
    vals = vals * np.repeat(np.exp2(scales.astype(np.float64) - 127.0), 8, axis=1)[..., None]
    return vals.transpose(0, 1, 3, 2).reshape(g * 512, n)


D, T, U, I, Q, E = 512, 1024, 1024, 512, 512, 256


def setup_inputs():
    n = np.random.standard_normal
    idx = np.stack([np.random.permutation(T)[:I] for _ in range(8)])
    idx2 = np.stack([np.random.permutation(U)[:I] for _ in range(8)])
    idx3 = np.stack([np.random.permutation(T)[:I] for _ in range(8)])
    idx4 = np.stack([np.random.permutation(T)[:I] for _ in range(8)])
    idx5 = np.stack([np.random.permutation(U)[:I] for _ in range(8)])
    fd = mx_kscale(D)
    fq = mx_kscale(Q)
    keysp = pack_weight(n((D, T)) / fd[:, None], "e2m1")
    notesp = pack_weight(n((D, U)) / fd[:, None], "e4m3")
    mixp = pack_weight(n((Q, E)) * 1.0 / np.sqrt(Q) / fq[:, None], "e4m3")
    return {
        "query": (n((D, Q)) * 1.0 / np.sqrt(D) * fd[:, None]).astype(np.float32),
        "query2": (n((D, Q)) * 1.0 / np.sqrt(D) * fd[:, None]).astype(np.float32),
        "keys_words": keysp[0],
        "keys_scales": keysp[1],
        "notes_words": notesp[0],
        "notes_scales": notesp[1],
        "rowf": (np.random.uniform(0.5, 2.0, (Q, 1)) * fq[:, None]).astype(np.float32),
        "mix_words": mixp[0],
        "mix_scales": mixp[1],
        "offs": striped8(idx),
        "offs2": striped8(idx2),
        "offs3": striped8(idx3),
        "offs4": striped8(idx4),
        "offs5": striped8(idx5),
    }


def reference(query, query2, keys_words, keys_scales, notes_words, notes_scales, rowf, mix_words, mix_scales, offs, offs2, offs3, offs4, offs5):
    idx = unstriped8(offs)
    idx2 = unstriped8(offs2)
    idx3 = unstriped8(offs3)
    idx4 = unstriped8(offs4)
    idx5 = unstriped8(offs5)
    keysu = unpack_weight(keys_words, keys_scales, "e2m1")
    notesu = unpack_weight(notes_words, notes_scales, "e4m3")
    mixu = unpack_weight(mix_words, mix_scales, "e4m3")
    queryq = mxq(f64(query), 0, "e4m3")
    a = queryq.T @ keysu
    query2q = mxq(f64(query2), 0, "e4m3")
    b = query2q.T @ notesu
    r = pick8(a, idx, 64) - pick8(b, idx2, 64)
    f1 = np.zeros((Q, T))
    f1[np.arange(Q)[:, None], idx3[np.arange(Q) % 512 // 64]] = r
    c1 = a + f1
    w = np.maximum(pick8(c1, idx4, 64), pick8(b, idx5, 64))
    g = w - r
    gw = g * f64(rowf)
    gwq = mxq(gw, 0, "e4m3")
    y = mixu.T @ gwq
    return y

@@ -1,0 +1,234 @@
+from contextlib import ExitStack
+
+import concourse.mybir as mybir
+
+D, T, U, I, Q, E = 512, 1024, 1024, 512, 512, 256
+FLOPS = 2 * D * Q * T + 2 * D * Q * U + 2 * Q * E * I
+
+F32 = mybir.dt.float32
+BF16 = mybir.dt.bfloat16
+I32 = mybir.dt.int32
+U32 = mybir.dt.uint32
+U16 = mybir.dt.uint16
+U8 = mybir.dt.uint8
+FP8X4 = mybir.dt.float8_e4m3fn_x4
+FP4X4 = mybir.dt.float4_e2m1fn_x4
+ALU = mybir.AluOpType
+COPY = mybir.ActivationFunctionType.Copy
+
+P = 128
+PACK = 4
+BANK = 512
+HALVES = 2
+
+
+def tile_attend_sidelooks_twoq_mixed_kernel(
+    tc, query, query2, keys_words, keys_scales, notes_words, notes_scales, rowf,
+    mix_words, mix_scales, offs, offs2, offs3, offs4, offs5, out,
+):
+    nc = tc.nc
+    with ExitStack() as ctx:
+        keep = ctx.enter_context(tc.tile_pool(name="keep", bufs=1))
+        psum = ctx.enter_context(tc.psum_pool(name="psum", bufs=2))
+
+        def scale_plane(name, width):
+            plane = keep.tile([P, width], U8, name=name, align_bytes=64)
+            nc.vector.memset(plane[:].bitcast(I32), 0)
+            return plane
+
+        def load_scale_rows(plane, scales):
+            for quad in range(4):
+                nc.sync.dma_start(
+                    plane[32 * quad : 32 * quad + 4, :].bitcast(I32),
+                    scales[0, 4 * quad : 4 * quad + 4, :].bitcast(I32),
+                )
+
+        def load_list(name, src):
+            lists = keep.tile([P, I // 16], U16, name=name)
+            nc.sync.dma_start(lists[:], src)
+            return lists
+
+        def load_query_half(name, src, h):
+            raw = keep.tile([P, 2, Q], F32, name=name)
+            nc.sync.dma_start(raw[:], src.rearrange("(p t) q -> p t q", t=PACK)[:, 2 * h : 2 * h + 2, :])
+            return raw
+
+        notes_plane = scale_plane("notes_plane", U)
+        keys_plane = scale_plane("keys_plane", T)
+        mix_plane = scale_plane("mix_plane", E)
+        f1 = [keep.tile([P, T], F32, name="f1_%d" % n) for n in range(2)]
+        for n in range(2):
+            nc.vector.memset(f1[n][:], 0.0)
+
+        q2_raw = [load_query_half("q2_raw%d" % h, query2, h) for h in range(HALVES)]
+        notes = keep.tile([P, U], U32, align_bytes=64)
+        nc.sync.dma_start(notes[:].bitcast(I32), notes_words[0].rearrange("p n t -> p (n t)").bitcast(I32))
+        load_scale_rows(notes_plane, notes_scales)
+        idx2 = load_list("idx2", offs2)
+        q_raw = [load_query_half("q_raw0", query, 0)]
+        idx5 = load_list("idx5", offs5)
+        q_raw.append(load_query_half("q_raw1", query, 1))
+        keys = keep.tile([P, 2 * T], U8, align_bytes=64)
+        nc.sync.dma_start(keys[:].bitcast(I32), keys_words[0].bitcast(I32))
+        load_scale_rows(keys_plane, keys_scales)
+        idx = load_list("idx", offs)
+        idx3 = load_list("idx3", offs3)
+        idx4 = load_list("idx4", offs4)
+        factor = keep.tile([P, PACK], F32)
+        nc.sync.dma_start(factor[:], rowf.rearrange("(p j) o -> p (j o)", j=PACK))
+        mix = keep.tile([P, E], U32, align_bytes=64)
+        nc.sync.dma_start(mix[:].bitcast(I32), mix_words[0].rearrange("p n t -> p (n t)").bitcast(I32))
+        load_scale_rows(mix_plane, mix_scales)
+
+        def quantise_queries(name, raw):
+            grouped = keep.tile([P, PACK, P, PACK], BF16, name=name + "_bf", align_bytes=64)
+            codes = keep.tile([P, PACK, P], U32, name=name + "_codes", align_bytes=64)
+            plane = keep.tile([P, PACK, P], U8, name=name + "_plane", align_bytes=64)
+            for h in range(HALVES):
+                nc.vector.tensor_copy(
+                    grouped[:, :, :, 2 * h : 2 * h + 2].rearrange("p j m t -> p m t j"),
+                    raw[h][:].rearrange("p t (m j) -> p m t j", j=PACK),
+                )
+            for j in range(PACK):
+                nc.vector.quantize_mx(
+                    codes[:, j, :].bitcast(FP8X4), plane[:, j, :],
+                    grouped[:, j, :, :].rearrange("p m t -> p (m t)"),
+                )
+            return codes, plane
+
+        def score_banks(qx, j, moving, moving_plane, pair):
+            banks = []
+            for n in range(2):
+                bank = psum.tile([P, BANK], F32, name="bank", tag="pair%d" % pair)
+                nc.tensor.matmul_mx(
+                    bank[:], lhsT=qx[0][:, j, :].bitcast(FP8X4), lhsT_scale=qx[1][:, j, :],
+                    rhs=moving(n), rhs_scale=moving_plane[:, n * BANK : (n + 1) * BANK],
+                    start=True, stop=True,
+                )
+                banks.append(bank)
+            return banks
+
+        def copy_out(engine, dst, src):
+            if engine == "S":
+                nc.scalar.copy(dst, src)
+            else:
+                nc.vector.tensor_copy(dst, src)
+
+        def empty(name, banks, engines):
+            scores = keep.tile([P, 2 * BANK], F32, name=name)
+            for n in range(2):
+                copy_out(engines[n], scores[:, n * BANK : (n + 1) * BANK], banks[n][:])
+            return scores
+
+        def look_up(tag, window, lists, engines="S"):
+            got = keep.tile([P, I], F32, name="got", tag=tag)
+            w = I // len(engines)
+            for h, engine in enumerate(engines):
+                listed = window[:].indirect(lists[:, h * w // 16 : (h + 1) * w // 16])
+                if engine == "S":
+                    nc.scalar.activation(got[:, h * w : (h + 1) * w], listed, COPY)
+                else:
+                    nc.vector.tensor_copy(got[:, h * w : (h + 1) * w], listed)
+            return got
+
+        def notes_moving(n):
+            return notes[:, n * BANK : (n + 1) * BANK].bitcast(FP8X4)
+
+        def keys_moving(n):
+            return keys[:, 2 * n * BANK : 2 * (n + 1) * BANK].bitcast(FP4X4)
+
+        gw_planes = keep.tile([P, PACK, I], BF16, align_bytes=64)
+        a, b, b2, r, c1, b5, c4, g = {}, {}, {}, {}, {}, {}, {}, {}
+        NOTE_PAIR = (0, 1, 2, 3)
+        TOKEN_PAIR = (2, 3, 0, 1)
+
+        def note_scores(j, engines):
+            b[j] = empty("b%d" % j, score_banks(q2x, j, notes_moving, notes_plane, NOTE_PAIR[j]), engines)
+
+        def token_scores(j, engines):
+            a[j] = empty("a%d" % j, score_banks(qx, j, keys_moving, keys_plane, TOKEN_PAIR[j]), engines)
+
+        def lead(j, engines):
+            a1 = look_up("side%d" % j, a[j], idx, engines)
+            r[j] = keep.tile([P, I], F32, name="r%d" % j)
+            nc.vector.tensor_tensor(r[j][:], a1[:], b2[j][:], ALU.subtract)
+
+        def place(j):
+            nc.vector.tensor_copy(f1[j % 2][:].indirect(idx3[:]), r[j][:])
+            c1[j] = keep.tile([P, T], F32, name="c1_%d" % j)
+            nc.vector.tensor_tensor(c1[j][:], a[j][:], f1[j % 2][:], ALU.add)
+
+        def rivals(j, engines):
+            b5[j] = look_up("side%d" % j, b[j], idx5)
+            c4[j] = look_up("c4_%d" % j, c1[j], idx4, engines)
+
+        def result(j, parts):
+            w = keep.tile([P, I], F32, name="w%d" % j)
+            g[j] = keep.tile([P, I], F32, name="g%d" % j)
+            width = I // parts
+            for h in range(parts):
+                cols = slice(h * width, (h + 1) * width)
+                nc.vector.tensor_tensor(w[:, cols], c4[j][:, cols], b5[j][:, cols], ALU.max)
+            for h in range(parts):
+                cols = slice(h * width, (h + 1) * width)
+                nc.vector.tensor_tensor(g[j][:, cols], w[:, cols], r[j][:, cols], ALU.subtract)
+
+        def weigh(j, parts):
+            width = I // parts
+            for h in range(parts):
+                cols = slice(h * width, (h + 1) * width)
+                nc.scalar.activation(gw_planes[:, j, cols], g[j][:, cols], COPY, scale=factor[:, j : j + 1])
+
+        q2x = quantise_queries("q2", q2_raw)
+        note_scores(0, "SS")
+        b2[0] = look_up("note_side", b[0], idx2)
+        note_scores(1, "VS")
+        qx = quantise_queries("q", q_raw)
+        token_scores(0, "SV")
+        lead(0, "SV")
+        place(0)
+        token_scores(1, "SS")
+        b2[1] = look_up("note_side", b[1], idx2)
+        lead(1, "S")
+        place(1)
+        note_scores(2, "SS")
+        token_scores(2, "SS")
+        b2[2] = look_up("note_side", b[2], idx2)
+        lead(2, "S")
+        place(2)
+        rivals(0, "S")
+        result(0, 1)
+        note_scores(3, "SS")
+        token_scores(3, "SS")
+        b2[3] = look_up("note_side", b[3], idx2)
+        lead(3, "S")
+        place(3)
+        weigh(0, 1)
+        rivals(1, "S")
+        rivals(2, "S")
+        rivals(3, "SS")
+        result(1, 1)
+        result(2, 1)
+        result(3, HALVES)
+        weigh(1, 1)
+        weigh(2, 1)
+        weigh(3, HALVES)
+
+        slots = I // HALVES
+        for h in range(HALVES):
+            cols = slice(h * slots, (h + 1) * slots)
+            woven = keep.tile([P, slots, PACK], BF16, name="woven%d" % h, align_bytes=64)
+            nc.vector.tensor_copy(woven[:], gw_planes[:, :, cols].rearrange("p j i -> p i j"))
+            codes = keep.tile([P, slots], U32, name="gw_codes%d" % h, align_bytes=64)
+            plane = keep.tile([P, slots], U8, name="gw_plane%d" % h, align_bytes=64)
+            nc.vector.quantize_mx(codes[:].bitcast(FP8X4), plane[:], woven[:].rearrange("p i j -> p (i j)"))
+            for eb in range(E // P):
+                ch = slice(eb * P, (eb + 1) * P)
+                bank = psum.tile([P, BANK], F32, name="bank", tag="pair%d" % h)
+                nc.tensor.matmul_mx(
+                    bank[:, :slots], lhsT=mix[:, ch].bitcast(FP8X4), lhsT_scale=mix_plane[:, ch],
+                    rhs=codes[:].bitcast(FP8X4), rhs_scale=plane[:], start=True, stop=True,
+                )
+                y = keep.tile([P, slots], F32, name="y%d_%d" % (h, eb))
+                copy_out("SV"[eb], y[:], bank[:, :slots])
+                nc.sync.dma_start(out[ch, cols], y[:])

@@ -120,8 +120,7 @@ def tile_attend_sidelooks_twoq_mixed_kernel(
                 copy_out(engines[n], scores[:, n * BANK : (n + 1) * BANK], banks[n][:])
             return scores
 
-        def look_up(tag, window, lists, engines="S"):
-            got = keep.tile([P, I], F32, name="got", tag=tag)
+        def look_up(got, window, lists, engines="S"):
             w = I // len(engines)
             for h, engine in enumerate(engines):
                 listed = window[:].indirect(lists[:, h * w // 16 : (h + 1) * w // 16])
@@ -129,7 +128,9 @@ def tile_attend_sidelooks_twoq_mixed_kernel(
                     nc.scalar.activation(got[:, h * w : (h + 1) * w], listed, COPY)
                 else:
                     nc.vector.tensor_copy(got[:, h * w : (h + 1) * w], listed)
-            return got
+
+        def slab(n):
+            return keep.tile([P, T], F32, name="slab", tag="slab%d" % (n % PACK))
 
         def notes_moving(n):
             return notes[:, n * BANK : (n + 1) * BANK].bitcast(FP8X4)
@@ -138,7 +139,7 @@ def tile_attend_sidelooks_twoq_mixed_kernel(
             return keys[:, 2 * n * BANK : 2 * (n + 1) * BANK].bitcast(FP4X4)
 
         gw_planes = keep.tile([P, PACK, I], BF16, align_bytes=64)
-        a, b, b2, r, c1, b5, c4, g = {}, {}, {}, {}, {}, {}, {}, {}
+        a, b, sides, r, c1, rivals, b5, w, g = {}, {}, {}, {}, {}, {}, {}, {}, {}
         NOTE_PAIR = (0, 1, 2, 3)
         TOKEN_PAIR = (2, 3, 0, 1)
 
@@ -148,71 +149,93 @@ def tile_attend_sidelooks_twoq_mixed_kernel(
         def token_scores(j, engines):
             a[j] = empty("a%d" % j, score_banks(qx, j, keys_moving, keys_plane, TOKEN_PAIR[j]), engines)
 
+        def note_side(j):
+            sides[j] = slab(j)
+            look_up(sides[j][:, I:], b[j], idx2)
+
         def lead(j, engines):
-            a1 = look_up("side%d" % j, a[j], idx, engines)
+            look_up(sides[j][:, :I], a[j], idx, engines)
             r[j] = keep.tile([P, I], F32, name="r%d" % j)
-            nc.vector.tensor_tensor(r[j][:], a1[:], b2[j][:], ALU.subtract)
+            nc.vector.tensor_tensor(r[j][:], sides[j][:, :I], sides[j][:, I:], ALU.subtract)
 
         def place(j):
             nc.vector.tensor_copy(f1[j % 2][:].indirect(idx3[:]), r[j][:])
-            c1[j] = keep.tile([P, T], F32, name="c1_%d" % j)
-            nc.vector.tensor_tensor(c1[j][:], a[j][:], f1[j % 2][:], ALU.add)
 
-        def rivals(j, engines):
-            b5[j] = look_up("side%d" % j, b[j], idx5)
-            c4[j] = look_up("c4_%d" % j, c1[j], idx4, engines)
+        def raise_scores(j):
+            c1[j] = slab(j + 1)
+            engine = nc.vector if j == PACK - 1 else nc.gpsimd
+            engine.tensor_tensor(c1[j][:], a[j][:], f1[j % 2][:], ALU.add)
 
-        def result(j, parts):
-            w = keep.tile([P, I], F32, name="w%d" % j)
-            g[j] = keep.tile([P, I], F32, name="g%d" % j)
-            width = I // parts
-            for h in range(parts):
-                cols = slice(h * width, (h + 1) * width)
-                nc.vector.tensor_tensor(w[:, cols], c4[j][:, cols], b5[j][:, cols], ALU.max)
-            for h in range(parts):
-                cols = slice(h * width, (h + 1) * width)
-                nc.vector.tensor_tensor(g[j][:, cols], w[:, cols], r[j][:, cols], ALU.subtract)
+        def note_rival(j):
+            if j == PACK - 1:
+                b5[j] = keep.tile([P, I], F32, name="last_rival")[:]
+                look_up(b5[j], b[j], idx5, "V")
+            else:
+                rivals[j] = slab(j)
+                b5[j] = rivals[j][:, I:]
+                look_up(b5[j], b[j], idx5)
 
-        def weigh(j, parts):
-            width = I // parts
-            for h in range(parts):
-                cols = slice(h * width, (h + 1) * width)
-                nc.scalar.activation(gw_planes[:, j, cols], g[j][:, cols], COPY, scale=factor[:, j : j + 1])
+        def token_rival(j, engines):
+            if j == PACK - 1:
+                rivals[j] = slab(j)
+            look_up(rivals[j][:, :I], c1[j], idx4, engines)
+
+        def larger(j, lo=0, hi=I):
+            if lo == 0:
+                w[j] = keep.tile([P, I], F32, name="w%d" % j)
+            nc.vector.tensor_tensor(w[j][:, lo:hi], rivals[j][:, lo:hi], b5[j][:, lo:hi], ALU.max)
+
+        def result(j, lo=0, hi=I):
+            if lo == 0:
+                g[j] = keep.tile([P, I], F32, name="g%d" % j)
+            nc.vector.tensor_tensor(g[j][:, lo:hi], w[j][:, lo:hi], r[j][:, lo:hi], ALU.subtract)
+
+        def weigh(j, lo=0, hi=I):
+            nc.scalar.activation(gw_planes[:, j, lo:hi], g[j][:, lo:hi], COPY, scale=factor[:, j : j + 1])
 
         q2x = quantise_queries("q2", q2_raw)
         note_scores(0, "SS")
-        b2[0] = look_up("note_side", b[0], idx2)
+        note_side(0)
         note_scores(1, "VS")
+        note_side(1)
         qx = quantise_queries("q", q_raw)
-        token_scores(0, "SV")
+        token_scores(0, "VV")
         lead(0, "SV")
         place(0)
         token_scores(1, "SS")
-        b2[1] = look_up("note_side", b[1], idx2)
         lead(1, "S")
+        raise_scores(0)
         place(1)
-        note_scores(2, "SS")
-        token_scores(2, "SS")
-        b2[2] = look_up("note_side", b[2], idx2)
-        lead(2, "S")
-        place(2)
-        rivals(0, "S")
-        result(0, 1)
-        note_scores(3, "SS")
-        token_scores(3, "SS")
-        b2[3] = look_up("note_side", b[3], idx2)
-        lead(3, "S")
-        place(3)
-        weigh(0, 1)
-        rivals(1, "S")
-        rivals(2, "S")
-        rivals(3, "SS")
-        result(1, 1)
-        result(2, 1)
-        result(3, HALVES)
-        weigh(1, 1)
-        weigh(2, 1)
-        weigh(3, HALVES)
+        for j in (2, 3):
+            note_scores(j, "SS")
+            token_scores(j, "SS")
+            note_side(j)
+            lead(j, "S")
+            raise_scores(j - 1)
+            place(j)
+        note_rival(0)
+        token_rival(0, "S")
+        larger(0)
+        raise_scores(3)
+        for j in (1, 2):
+            note_rival(j)
+            token_rival(j, "S")
+        note_rival(3)
+        token_rival(3, "SS")
+        mid = I // HALVES
+        larger(1)
+        result(0)
+        result(1)
+        larger(2)
+        larger(3, 0, mid)
+        result(2)
+        larger(3, mid, I)
+        result(3, 0, mid)
+        result(3, mid, I)
+        for j in range(3):
+            weigh(j)
+        weigh(3, 0, mid)
+        weigh(3, mid, I)
 
         slots = I // HALVES
         for h in range(HALVES):

@@ -18,8 +18,13 @@ COPY = mybir.ActivationFunctionType.Copy
 
 P = 128
 PACK = 4
+LAST = PACK - 1
 BANK = 512
-HALVES = 2
+LIST_ROWS = 16
+MID = I // 2
+VECTOR_CAST = 88
+VECTOR_TOKEN_TILE = 2
+VECTOR, SCALAR = "vector", "scalar"
 
 
 def tile_attend_sidelooks_twoq_mixed_kernel(
@@ -31,64 +36,70 @@ def tile_attend_sidelooks_twoq_mixed_kernel(
         keep = ctx.enter_context(tc.tile_pool(name="keep", bufs=1))
         psum = ctx.enter_context(tc.psum_pool(name="psum", bufs=2))
 
-        def scale_plane(name, width):
+        def zeroed_plane(name, width):
             plane = keep.tile([P, width], U8, name=name, align_bytes=64)
             nc.vector.memset(plane[:].bitcast(I32), 0)
             return plane
 
         def load_scale_rows(plane, scales):
-            for quad in range(4):
+            for n in range(4):
                 nc.sync.dma_start(
-                    plane[32 * quad : 32 * quad + 4, :].bitcast(I32),
-                    scales[0, 4 * quad : 4 * quad + 4, :].bitcast(I32),
+                    plane[32 * n : 32 * n + 4, :].bitcast(I32),
+                    scales[0, 4 * n : 4 * n + 4, :].bitcast(I32),
                 )
 
-        def load_list(name, src):
-            lists = keep.tile([P, I // 16], U16, name=name)
+        def load_lists(name, src):
+            lists = keep.tile([P, I // LIST_ROWS], U16, name=name)
             nc.sync.dma_start(lists[:], src)
             return lists
 
-        def load_query_half(name, src, h):
+        def load_feature_pair(name, src, u):
             raw = keep.tile([P, 2, Q], F32, name=name)
-            nc.sync.dma_start(raw[:], src.rearrange("(p t) q -> p t q", t=PACK)[:, 2 * h : 2 * h + 2, :])
+            nc.sync.dma_start(raw[:], src.rearrange("(p t) q -> p t q", t=PACK)[:, 2 * u : 2 * u + 2, :])
             return raw
 
-        notes_plane = scale_plane("notes_plane", U)
-        keys_plane = scale_plane("keys_plane", T)
-        mix_plane = scale_plane("mix_plane", E)
+        keys_plane = zeroed_plane("keys_plane", T)
+        notes_plane = zeroed_plane("notes_plane", U)
+        mix_plane = zeroed_plane("mix_plane", E)
         f1 = [keep.tile([P, T], F32, name="f1_%d" % n) for n in range(2)]
-        for n in range(2):
-            nc.vector.memset(f1[n][:], 0.0)
+        for window in f1:
+            nc.vector.memset(window[:], 0.0)
 
-        q2_raw = [load_query_half("q2_raw%d" % h, query2, h) for h in range(HALVES)]
-        notes = keep.tile([P, U], U32, align_bytes=64)
-        nc.sync.dma_start(notes[:].bitcast(I32), notes_words[0].rearrange("p n t -> p (n t)").bitcast(I32))
-        load_scale_rows(notes_plane, notes_scales)
-        idx2 = load_list("idx2", offs2)
-        q_raw = [load_query_half("q_raw0", query, 0)]
-        idx5 = load_list("idx5", offs5)
-        q_raw.append(load_query_half("q_raw1", query, 1))
+        q_raw = [load_feature_pair("q_raw%d" % u, query, u) for u in range(2)]
         keys = keep.tile([P, 2 * T], U8, align_bytes=64)
         nc.sync.dma_start(keys[:].bitcast(I32), keys_words[0].bitcast(I32))
         load_scale_rows(keys_plane, keys_scales)
-        idx = load_list("idx", offs)
-        idx3 = load_list("idx3", offs3)
-        idx4 = load_list("idx4", offs4)
+        q2_raw = [load_feature_pair("q2_raw0", query2, 0)]
+        idx = load_lists("idx", offs)
+        q2_raw.append(load_feature_pair("q2_raw1", query2, 1))
+        notes = keep.tile([P, U], U32, align_bytes=64)
+        nc.sync.dma_start(notes[:].bitcast(I32), notes_words[0].rearrange("p n t -> p (n t)").bitcast(I32))
+        load_scale_rows(notes_plane, notes_scales)
+        idx2 = load_lists("idx2", offs2)
+        idx3 = load_lists("idx3", offs3)
+        idx5 = load_lists("idx5", offs5)
+        idx4 = load_lists("idx4", offs4)
         factor = keep.tile([P, PACK], F32)
         nc.sync.dma_start(factor[:], rowf.rearrange("(p j) o -> p (j o)", j=PACK))
         mix = keep.tile([P, E], U32, align_bytes=64)
         nc.sync.dma_start(mix[:].bitcast(I32), mix_words[0].rearrange("p n t -> p (n t)").bitcast(I32))
         load_scale_rows(mix_plane, mix_scales)
 
-        def quantise_queries(name, raw):
+        def copy(engine, dst, src):
+            if engine == SCALAR:
+                nc.scalar.copy(dst, src)
+            else:
+                nc.vector.tensor_copy(dst, src)
+
+        def quantise_queries(name, raw, shares):
             grouped = keep.tile([P, PACK, P, PACK], BF16, name=name + "_bf", align_bytes=64)
             codes = keep.tile([P, PACK, P], U32, name=name + "_codes", align_bytes=64)
             plane = keep.tile([P, PACK, P], U8, name=name + "_plane", align_bytes=64)
-            for h in range(HALVES):
-                nc.vector.tensor_copy(
-                    grouped[:, :, :, 2 * h : 2 * h + 2].rearrange("p j m t -> p m t j"),
-                    raw[h][:].rearrange("p t (m j) -> p m t j", j=PACK),
-                )
+            for u in range(2):
+                dst = grouped[:, :, :, 2 * u : 2 * u + 2].rearrange("p j m t -> p m t j")
+                src = raw[u][:].rearrange("p t (m j) -> p m t j", j=PACK)
+                for engine, lo, hi in shares:
+                    copy(engine, dst[:, lo:hi], src[:, lo:hi])
             for j in range(PACK):
                 nc.vector.quantize_mx(
                     codes[:, j, :].bitcast(FP8X4), plane[:, j, :],
@@ -96,162 +107,135 @@ def tile_attend_sidelooks_twoq_mixed_kernel(
                 )
             return codes, plane
 
-        def score_banks(qx, j, moving, moving_plane, pair):
+        def scores(name, queries, j, moving, moving_plane, pair, engine):
+            codes, plane = queries
             banks = []
             for n in range(2):
                 bank = psum.tile([P, BANK], F32, name="bank", tag="pair%d" % pair)
                 nc.tensor.matmul_mx(
-                    bank[:], lhsT=qx[0][:, j, :].bitcast(FP8X4), lhsT_scale=qx[1][:, j, :],
-                    rhs=moving(n), rhs_scale=moving_plane[:, n * BANK : (n + 1) * BANK],
+                    bank[:], lhsT=codes[:, j, :].bitcast(FP8X4), lhsT_scale=plane[:, j, :],
+                    rhs=moving[n], rhs_scale=moving_plane[:, n * BANK : (n + 1) * BANK],
                     start=True, stop=True,
                 )
                 banks.append(bank)
-            return banks
-
-        def copy_out(engine, dst, src):
-            if engine == "S":
-                nc.scalar.copy(dst, src)
-            else:
-                nc.vector.tensor_copy(dst, src)
-
-        def empty(name, banks, engines):
-            scores = keep.tile([P, 2 * BANK], F32, name=name)
+            table = keep.tile([P, 2 * BANK], F32, name=name)
             for n in range(2):
-                copy_out(engines[n], scores[:, n * BANK : (n + 1) * BANK], banks[n][:])
-            return scores
+                copy(engine, table[:, n * BANK : (n + 1) * BANK], banks[n][:])
+            return table
 
-        def look_up(got, window, lists, engines="S"):
-            w = I // len(engines)
-            for h, engine in enumerate(engines):
-                listed = window[:].indirect(lists[:, h * w // 16 : (h + 1) * w // 16])
-                if engine == "S":
-                    nc.scalar.activation(got[:, h * w : (h + 1) * w], listed, COPY)
+        def look_up(got, window, lists, engines):
+            width = I // len(engines)
+            for n, engine in enumerate(engines):
+                dst = got[:, n * width : (n + 1) * width]
+                listed = window[:].indirect(lists[:, n * width // LIST_ROWS : (n + 1) * width // LIST_ROWS])
+                if engine == SCALAR:
+                    nc.scalar.activation(dst, listed, COPY)
                 else:
-                    nc.vector.tensor_copy(got[:, h * w : (h + 1) * w], listed)
+                    nc.vector.tensor_copy(dst, listed)
 
         def slab(n):
             return keep.tile([P, T], F32, name="slab", tag="slab%d" % (n % PACK))
 
-        def notes_moving(n):
-            return notes[:, n * BANK : (n + 1) * BANK].bitcast(FP8X4)
+        keys_moving = [keys[:, 2 * n * BANK : 2 * (n + 1) * BANK].bitcast(FP4X4) for n in range(2)]
+        notes_moving = [notes[:, n * BANK : (n + 1) * BANK].bitcast(FP8X4) for n in range(2)]
 
-        def keys_moving(n):
-            return keys[:, 2 * n * BANK : 2 * (n + 1) * BANK].bitcast(FP4X4)
+        gw_rows = keep.tile([P, PACK, I], BF16, align_bytes=64)
+        a, b, sides, r, c1, c4, b5, w, g = {}, {}, {}, {}, {}, {}, {}, {}, {}
 
-        gw_planes = keep.tile([P, PACK, I], BF16, align_bytes=64)
-        a, b, sides, r, c1, rivals, b5, w, g = {}, {}, {}, {}, {}, {}, {}, {}, {}
-        NOTE_PAIR = (0, 1, 2, 3)
-        TOKEN_PAIR = (2, 3, 0, 1)
+        def token_scores(j):
+            a[j] = scores("a%d" % j, qx, j, keys_moving, keys_plane, j, SCALAR)
 
-        def note_scores(j, engines):
-            b[j] = empty("b%d" % j, score_banks(q2x, j, notes_moving, notes_plane, NOTE_PAIR[j]), engines)
+        def note_scores(j, engine):
+            b[j] = scores("b%d" % j, q2x, j, notes_moving, notes_plane, (j + 2) % PACK, engine)
 
-        def token_scores(j, engines):
-            a[j] = empty("a%d" % j, score_banks(qx, j, keys_moving, keys_plane, TOKEN_PAIR[j]), engines)
-
-        def note_side(j):
+        def token_side(j):
             sides[j] = slab(j)
-            look_up(sides[j][:, I:], b[j], idx2)
+            look_up(sides[j][:, :I], a[j], idx, [VECTOR if j == VECTOR_TOKEN_TILE else SCALAR])
 
-        def lead(j, engines):
-            look_up(sides[j][:, :I], a[j], idx, engines)
+        def lead(j, engine):
+            look_up(sides[j][:, I:], b[j], idx2, [engine])
             r[j] = keep.tile([P, I], F32, name="r%d" % j)
             nc.vector.tensor_tensor(r[j][:], sides[j][:, :I], sides[j][:, I:], ALU.subtract)
 
         def place(j):
             nc.vector.tensor_copy(f1[j % 2][:].indirect(idx3[:]), r[j][:])
 
-        def raise_scores(j):
+        def add_lead(j, engine):
             c1[j] = slab(j + 1)
-            engine = nc.vector if j == PACK - 1 else nc.gpsimd
             engine.tensor_tensor(c1[j][:], a[j][:], f1[j % 2][:], ALU.add)
 
-        def note_rival(j):
-            if j == PACK - 1:
-                b5[j] = keep.tile([P, I], F32, name="last_rival")[:]
-                look_up(b5[j], b[j], idx5, "V")
-            else:
-                rivals[j] = slab(j)
-                b5[j] = rivals[j][:, I:]
-                look_up(b5[j], b[j], idx5)
+        def rivals(j, b5_tile, b5_engines, c4_tile, c4_engines):
+            b5[j], c4[j] = b5_tile, c4_tile
+            look_up(b5[j], b[j], idx5, b5_engines)
+            look_up(c4[j], c1[j], idx4, c4_engines)
 
-        def token_rival(j, engines):
-            if j == PACK - 1:
-                rivals[j] = slab(j)
-            look_up(rivals[j][:, :I], c1[j], idx4, engines)
+        def own_tile(name):
+            return keep.tile([P, I], F32, name=name)[:]
 
-        def larger(j, lo=0, hi=I):
-            if lo == 0:
-                w[j] = keep.tile([P, I], F32, name="w%d" % j)
-            nc.vector.tensor_tensor(w[j][:, lo:hi], rivals[j][:, lo:hi], b5[j][:, lo:hi], ALU.max)
+        def larger(j, cols):
+            nc.vector.tensor_tensor(w[j][:, cols], c4[j][:, cols], b5[j][:, cols], ALU.max)
 
-        def result(j, lo=0, hi=I):
-            if lo == 0:
-                g[j] = keep.tile([P, I], F32, name="g%d" % j)
-            nc.vector.tensor_tensor(g[j][:, lo:hi], w[j][:, lo:hi], r[j][:, lo:hi], ALU.subtract)
+        def less_lead(j, cols):
+            nc.vector.tensor_tensor(g[j][:, cols], w[j][:, cols], r[j][:, cols], ALU.subtract)
 
-        def weigh(j, lo=0, hi=I):
-            nc.scalar.activation(gw_planes[:, j, lo:hi], g[j][:, lo:hi], COPY, scale=factor[:, j : j + 1])
-
-        q2x = quantise_queries("q2", q2_raw)
-        note_scores(0, "SS")
-        note_side(0)
-        note_scores(1, "VS")
-        note_side(1)
-        qx = quantise_queries("q", q_raw)
-        token_scores(0, "VV")
-        lead(0, "SV")
+        qx = quantise_queries("q", q_raw, [(VECTOR, 0, VECTOR_CAST), (SCALAR, VECTOR_CAST, P)])
+        token_scores(0)
+        token_side(0)
+        q2x = quantise_queries("q2", q2_raw, [(VECTOR, 0, P)])
+        note_scores(0, VECTOR)
+        token_scores(1)
+        token_side(1)
+        lead(0, VECTOR)
         place(0)
-        token_scores(1, "SS")
-        lead(1, "S")
-        raise_scores(0)
-        place(1)
-        for j in (2, 3):
-            note_scores(j, "SS")
-            token_scores(j, "SS")
-            note_side(j)
-            lead(j, "S")
-            raise_scores(j - 1)
+        for j in range(1, PACK):
+            note_scores(j, SCALAR)
+            if j not in a:
+                token_scores(j)
+                token_side(j)
+            lead(j, SCALAR)
+            add_lead(j - 1, nc.gpsimd)
             place(j)
-        note_rival(0)
-        token_rival(0, "S")
-        larger(0)
-        raise_scores(3)
-        for j in (1, 2):
-            note_rival(j)
-            token_rival(j, "S")
-        note_rival(3)
-        token_rival(3, "SS")
-        mid = I // HALVES
-        larger(1)
-        result(0)
-        result(1)
-        larger(2)
-        larger(3, 0, mid)
-        result(2)
-        larger(3, mid, I)
-        result(3, 0, mid)
-        result(3, mid, I)
-        for j in range(3):
-            weigh(j)
-        weigh(3, 0, mid)
-        weigh(3, mid, I)
 
-        slots = I // HALVES
-        for h in range(HALVES):
-            cols = slice(h * slots, (h + 1) * slots)
-            woven = keep.tile([P, slots, PACK], BF16, name="woven%d" % h, align_bytes=64)
-            nc.vector.tensor_copy(woven[:], gw_planes[:, :, cols].rearrange("p j i -> p i j"))
-            codes = keep.tile([P, slots], U32, name="gw_codes%d" % h, align_bytes=64)
-            plane = keep.tile([P, slots], U8, name="gw_plane%d" % h, align_bytes=64)
-            nc.vector.quantize_mx(codes[:].bitcast(FP8X4), plane[:], woven[:].rearrange("p i j -> p (i j)"))
-            for eb in range(E // P):
-                ch = slice(eb * P, (eb + 1) * P)
+        for j in range(PACK):
+            w[j], g[j] = own_tile("w%d" % j), own_tile("g%d" % j)
+        whole, first, second = slice(0, I), slice(0, MID), slice(MID, I)
+
+        both = slab(0)
+        rivals(0, both[:, I:], [SCALAR], both[:, :I], [SCALAR])
+        larger(0, whole)
+        add_lead(LAST, nc.vector)
+        for j in range(1, LAST):
+            rivals(j, own_tile("b5_%d" % j), [SCALAR], slab(j)[:, :I], [SCALAR])
+        rivals(LAST, own_tile("b5_last"), [SCALAR, VECTOR], slab(LAST)[:, :I], [SCALAR, SCALAR])
+
+        larger(1, whole)
+        less_lead(0, whole)
+        less_lead(1, whole)
+        larger(2, whole)
+        larger(LAST, first)
+        less_lead(2, whole)
+        larger(LAST, second)
+        less_lead(LAST, first)
+        less_lead(LAST, second)
+
+        for j in range(LAST):
+            nc.scalar.activation(gw_rows[:, j, :], g[j], COPY, scale=factor[:, j : j + 1])
+        for cols in (first, second):
+            nc.vector.tensor_scalar_mul(gw_rows[:, LAST, cols], g[LAST][:, cols], factor[:, LAST : LAST + 1])
+
+        for h, cols in enumerate((first, second)):
+            woven = keep.tile([P, MID, PACK], BF16, name="woven%d" % h, align_bytes=64)
+            copy((VECTOR, SCALAR)[h], woven[:], gw_rows[:, :, cols].rearrange("p j i -> p i j"))
+            gw_codes = keep.tile([P, MID], U32, name="gw_codes%d" % h, align_bytes=64)
+            gw_plane = keep.tile([P, MID], U8, name="gw_plane%d" % h, align_bytes=64)
+            nc.vector.quantize_mx(gw_codes[:].bitcast(FP8X4), gw_plane[:], woven[:].rearrange("p i j -> p (i j)"))
+            for block in range(E // P):
+                channels = slice(block * P, (block + 1) * P)
                 bank = psum.tile([P, BANK], F32, name="bank", tag="pair%d" % h)
                 nc.tensor.matmul_mx(
-                    bank[:, :slots], lhsT=mix[:, ch].bitcast(FP8X4), lhsT_scale=mix_plane[:, ch],
-                    rhs=codes[:].bitcast(FP8X4), rhs_scale=plane[:], start=True, stop=True,
+                    bank[:, :MID], lhsT=mix[:, channels].bitcast(FP8X4), lhsT_scale=mix_plane[:, channels],
+                    rhs=gw_codes[:].bitcast(FP8X4), rhs_scale=gw_plane[:], start=True, stop=True,
                 )
-                y = keep.tile([P, slots], F32, name="y%d_%d" % (h, eb))
-                copy_out("SV"[eb], y[:], bank[:, :slots])
-                nc.sync.dma_start(out[ch, cols], y[:])
+                y = keep.tile([P, MID], F32, name="y%d_%d" % (h, block))
+                copy((SCALAR, VECTOR)[block], y[:], bank[:, :MID])
+                (nc.scalar, nc.sync)[block].dma_start(out[channels, cols], y[:])

from contextlib import ExitStack

import concourse.mybir as mybir

D, T, U, I, Q, E = 512, 1024, 1024, 512, 512, 256
FLOPS = 2 * D * Q * T + 2 * D * Q * U + 2 * Q * E * I

F32 = mybir.dt.float32
BF16 = mybir.dt.bfloat16
I32 = mybir.dt.int32
U32 = mybir.dt.uint32
U16 = mybir.dt.uint16
U8 = mybir.dt.uint8
FP8X4 = mybir.dt.float8_e4m3fn_x4
FP4X4 = mybir.dt.float4_e2m1fn_x4
ALU = mybir.AluOpType
COPY = mybir.ActivationFunctionType.Copy

P = 128
PACK = 4
LAST = PACK - 1
BANK = 512
LIST_ROWS = 16
MID = I // 2
VECTOR_CAST = 88
VECTOR_TOKEN_TILE = 2
VECTOR, SCALAR = "vector", "scalar"


def tile_attend_sidelooks_twoq_mixed_kernel(
    tc, query, query2, keys_words, keys_scales, notes_words, notes_scales, rowf,
    mix_words, mix_scales, offs, offs2, offs3, offs4, offs5, out,
):
    nc = tc.nc
    with ExitStack() as ctx:
        keep = ctx.enter_context(tc.tile_pool(name="keep", bufs=1))
        psum = ctx.enter_context(tc.psum_pool(name="psum", bufs=2))

        def zeroed_plane(name, width):
            plane = keep.tile([P, width], U8, name=name, align_bytes=64)
            nc.vector.memset(plane[:].bitcast(I32), 0)
            return plane

        def load_scale_rows(plane, scales):
            for n in range(4):
                nc.sync.dma_start(
                    plane[32 * n : 32 * n + 4, :].bitcast(I32),
                    scales[0, 4 * n : 4 * n + 4, :].bitcast(I32),
                )

        def load_lists(name, src):
            lists = keep.tile([P, I // LIST_ROWS], U16, name=name)
            nc.sync.dma_start(lists[:], src)
            return lists

        def load_feature_pair(name, src, u):
            raw = keep.tile([P, 2, Q], F32, name=name)
            nc.sync.dma_start(raw[:], src.rearrange("(p t) q -> p t q", t=PACK)[:, 2 * u : 2 * u + 2, :])
            return raw

        keys_plane = zeroed_plane("keys_plane", T)
        notes_plane = zeroed_plane("notes_plane", U)
        mix_plane = zeroed_plane("mix_plane", E)
        f1 = [keep.tile([P, T], F32, name="f1_%d" % n) for n in range(2)]
        for window in f1:
            nc.vector.memset(window[:], 0.0)

        q_raw = [load_feature_pair("q_raw%d" % u, query, u) for u in range(2)]
        keys = keep.tile([P, 2 * T], U8, align_bytes=64)
        nc.sync.dma_start(keys[:].bitcast(I32), keys_words[0].bitcast(I32))
        load_scale_rows(keys_plane, keys_scales)
        q2_raw = [load_feature_pair("q2_raw0", query2, 0)]
        idx = load_lists("idx", offs)
        q2_raw.append(load_feature_pair("q2_raw1", query2, 1))
        notes = keep.tile([P, U], U32, align_bytes=64)
        nc.sync.dma_start(notes[:].bitcast(I32), notes_words[0].rearrange("p n t -> p (n t)").bitcast(I32))
        load_scale_rows(notes_plane, notes_scales)
        idx2 = load_lists("idx2", offs2)
        idx3 = load_lists("idx3", offs3)
        idx5 = load_lists("idx5", offs5)
        idx4 = load_lists("idx4", offs4)
        factor = keep.tile([P, PACK], F32)
        nc.sync.dma_start(factor[:], rowf.rearrange("(p j) o -> p (j o)", j=PACK))
        mix = keep.tile([P, E], U32, align_bytes=64)
        nc.sync.dma_start(mix[:].bitcast(I32), mix_words[0].rearrange("p n t -> p (n t)").bitcast(I32))
        load_scale_rows(mix_plane, mix_scales)

        def copy(engine, dst, src):
            if engine == SCALAR:
                nc.scalar.copy(dst, src)
            else:
                nc.vector.tensor_copy(dst, src)

        def quantise_queries(name, raw, shares):
            grouped = keep.tile([P, PACK, P, PACK], BF16, name=name + "_bf", align_bytes=64)
            codes = keep.tile([P, PACK, P], U32, name=name + "_codes", align_bytes=64)
            plane = keep.tile([P, PACK, P], U8, name=name + "_plane", align_bytes=64)
            for u in range(2):
                dst = grouped[:, :, :, 2 * u : 2 * u + 2].rearrange("p j m t -> p m t j")
                src = raw[u][:].rearrange("p t (m j) -> p m t j", j=PACK)
                for engine, lo, hi in shares:
                    copy(engine, dst[:, lo:hi], src[:, lo:hi])
            for j in range(PACK):
                nc.vector.quantize_mx(
                    codes[:, j, :].bitcast(FP8X4), plane[:, j, :],
                    grouped[:, j, :, :].rearrange("p m t -> p (m t)"),
                )
            return codes, plane

        def scores(name, queries, j, moving, moving_plane, pair, engine):
            codes, plane = queries
            banks = []
            for n in range(2):
                bank = psum.tile([P, BANK], F32, name="bank", tag="pair%d" % pair)
                nc.tensor.matmul_mx(
                    bank[:], lhsT=codes[:, j, :].bitcast(FP8X4), lhsT_scale=plane[:, j, :],
                    rhs=moving[n], rhs_scale=moving_plane[:, n * BANK : (n + 1) * BANK],
                    start=True, stop=True,
                )
                banks.append(bank)
            table = keep.tile([P, 2 * BANK], F32, name=name)
            for n in range(2):
                copy(engine, table[:, n * BANK : (n + 1) * BANK], banks[n][:])
            return table

        def look_up(got, window, lists, engines):
            width = I // len(engines)
            for n, engine in enumerate(engines):
                dst = got[:, n * width : (n + 1) * width]
                listed = window[:].indirect(lists[:, n * width // LIST_ROWS : (n + 1) * width // LIST_ROWS])
                if engine == SCALAR:
                    nc.scalar.activation(dst, listed, COPY)
                else:
                    nc.vector.tensor_copy(dst, listed)

        def slab(n):
            return keep.tile([P, T], F32, name="slab", tag="slab%d" % (n % PACK))

        keys_moving = [keys[:, 2 * n * BANK : 2 * (n + 1) * BANK].bitcast(FP4X4) for n in range(2)]
        notes_moving = [notes[:, n * BANK : (n + 1) * BANK].bitcast(FP8X4) for n in range(2)]

        gw_rows = keep.tile([P, PACK, I], BF16, align_bytes=64)
        a, b, sides, r, c1, c4, b5, w, g = {}, {}, {}, {}, {}, {}, {}, {}, {}

        def token_scores(j):
            a[j] = scores("a%d" % j, qx, j, keys_moving, keys_plane, j, SCALAR)

        def note_scores(j, engine):
            b[j] = scores("b%d" % j, q2x, j, notes_moving, notes_plane, (j + 2) % PACK, engine)

        def token_side(j):
            sides[j] = slab(j)
            look_up(sides[j][:, :I], a[j], idx, [VECTOR if j == VECTOR_TOKEN_TILE else SCALAR])

        def lead(j, engine):
            look_up(sides[j][:, I:], b[j], idx2, [engine])
            r[j] = keep.tile([P, I], F32, name="r%d" % j)
            nc.vector.tensor_tensor(r[j][:], sides[j][:, :I], sides[j][:, I:], ALU.subtract)

        def place(j):
            nc.vector.tensor_copy(f1[j % 2][:].indirect(idx3[:]), r[j][:])

        def add_lead(j, engine):
            c1[j] = slab(j + 1)
            engine.tensor_tensor(c1[j][:], a[j][:], f1[j % 2][:], ALU.add)

        def rivals(j, b5_tile, b5_engines, c4_tile, c4_engines):
            b5[j], c4[j] = b5_tile, c4_tile
            look_up(b5[j], b[j], idx5, b5_engines)
            look_up(c4[j], c1[j], idx4, c4_engines)

        def own_tile(name):
            return keep.tile([P, I], F32, name=name)[:]

        def larger(j, cols):
            nc.vector.tensor_tensor(w[j][:, cols], c4[j][:, cols], b5[j][:, cols], ALU.max)

        def less_lead(j, cols):
            nc.vector.tensor_tensor(g[j][:, cols], w[j][:, cols], r[j][:, cols], ALU.subtract)

        qx = quantise_queries("q", q_raw, [(VECTOR, 0, VECTOR_CAST), (SCALAR, VECTOR_CAST, P)])
        token_scores(0)
        token_side(0)
        q2x = quantise_queries("q2", q2_raw, [(VECTOR, 0, P)])
        note_scores(0, VECTOR)
        token_scores(1)
        token_side(1)
        lead(0, VECTOR)
        place(0)
        for j in range(1, PACK):
            note_scores(j, SCALAR)
            if j not in a:
                token_scores(j)
                token_side(j)
            lead(j, SCALAR)
            add_lead(j - 1, nc.gpsimd)
            place(j)

        for j in range(PACK):
            w[j], g[j] = own_tile("w%d" % j), own_tile("g%d" % j)
        whole, first, second = slice(0, I), slice(0, MID), slice(MID, I)

        both = slab(0)
        rivals(0, both[:, I:], [SCALAR], both[:, :I], [SCALAR])
        larger(0, whole)
        add_lead(LAST, nc.vector)
        for j in range(1, LAST):
            rivals(j, own_tile("b5_%d" % j), [SCALAR], slab(j)[:, :I], [SCALAR])
        rivals(LAST, own_tile("b5_last"), [SCALAR, VECTOR], slab(LAST)[:, :I], [SCALAR, SCALAR])

        larger(1, whole)
        less_lead(0, whole)
        less_lead(1, whole)
        larger(2, whole)
        larger(LAST, first)
        less_lead(2, whole)
        larger(LAST, second)
        less_lead(LAST, first)
        less_lead(LAST, second)

        for j in range(LAST):
            nc.scalar.activation(gw_rows[:, j, :], g[j], COPY, scale=factor[:, j : j + 1])
        for cols in (first, second):
            nc.vector.tensor_scalar_mul(gw_rows[:, LAST, cols], g[LAST][:, cols], factor[:, LAST : LAST + 1])

        for h, cols in enumerate((first, second)):
            woven = keep.tile([P, MID, PACK], BF16, name="woven%d" % h, align_bytes=64)
            copy((VECTOR, SCALAR)[h], woven[:], gw_rows[:, :, cols].rearrange("p j i -> p i j"))
            gw_codes = keep.tile([P, MID], U32, name="gw_codes%d" % h, align_bytes=64)
            gw_plane = keep.tile([P, MID], U8, name="gw_plane%d" % h, align_bytes=64)
            nc.vector.quantize_mx(gw_codes[:].bitcast(FP8X4), gw_plane[:], woven[:].rearrange("p i j -> p (i j)"))
            for block in range(E // P):
                channels = slice(block * P, (block + 1) * P)
                bank = psum.tile([P, BANK], F32, name="bank", tag="pair%d" % h)
                nc.tensor.matmul_mx(
                    bank[:, :MID], lhsT=mix[:, channels].bitcast(FP8X4), lhsT_scale=mix_plane[:, channels],
                    rhs=gw_codes[:].bitcast(FP8X4), rhs_scale=gw_plane[:], start=True, stop=True,
                )
                y = keep.tile([P, MID], F32, name="y%d_%d" % (h, block))
                copy((SCALAR, VECTOR)[block], y[:], bank[:, :MID])
                (nc.scalar, nc.sync)[block].dma_start(out[channels, cols], y[:])
